import numpy as np
import ml_dtypes


def mxq(x, axis, fmt="e4m3"):
    dtype, down = {"e4m3": (ml_dtypes.float8_e4m3fn, 7), "e5m2": (ml_dtypes.float8_e5m2, 14)}[fmt]
    v = np.moveaxis(np.asarray(x, np.float32).astype(ml_dtypes.bfloat16).astype(np.float64), axis, -1)
    blocks = v.reshape(v.shape[:-1] + (-1, 32))
    amax = np.abs(blocks).max(-1, keepdims=True)
    byte = np.maximum(np.where(amax > 0, np.frexp(amax)[1] - 1 + 127, 0) - down, 1)
    scale = np.exp2(byte - 127.0)
    codes = (blocks / scale).astype(np.float32).astype(dtype).astype(np.float64)
    return np.moveaxis((codes * scale).reshape(v.shape), -1, axis)


WIDE = False


def mx_kscale(k):
    if not WIDE:
        return np.ones(k)
    levels = np.array([10, -10, 5, -5, 0])
    if k % 512:
        return np.exp2(np.random.permutation(np.resize(levels, k // 32))).repeat(32)
    a = np.empty((k // 512, 16))
    for p in range(k // 512):
        a[p, :8] = np.random.permutation(np.resize(levels, 8))
        for g in range(8):
            far = levels[np.abs(levels - a[p, g]) >= 10]
            a[p, g + 8] = far[np.random.randint(len(far))]
    return np.exp2(a.ravel()).repeat(32)


def f64(x):
    return np.asarray(x).astype(np.float64)


def striped(idx):
    return np.tile(idx.reshape(-1, 16).T, (8, 1)).astype(np.uint16)


def unstriped(offs):
    return offs[:16].T.reshape(-1).astype(np.int64)


def pack_weight(w):
    k, n = w.shape
    w = f64(np.asarray(w, np.float32).astype(ml_dtypes.bfloat16)).reshape(k // 32, 32, n)
    amax = np.abs(w).max(1)
    byte = np.clip(np.where(amax > 0, np.frexp(amax)[1] - 1 + 127 - 7, 1), 1, 254)
    scaled = (w * np.exp2(127.0 - byte)[:, None, :]).reshape(k, n).astype(np.float32)
    words = np.ascontiguousarray(scaled.reshape(k // 512, 128, 4, n).transpose(0, 1, 3, 2)).astype(ml_dtypes.float8_e4m3fn).view(np.uint8)
    return words, np.ascontiguousarray(byte.astype(np.uint8).reshape(k // 512, 16, n))


def unpack_weight(words, scales):
    g, p, n, _ = words.shape
    vals = np.ascontiguousarray(words).view(ml_dtypes.float8_e4m3fn).astype(np.float64) * np.repeat(np.exp2(scales.astype(np.float64) - 127.0), 8, axis=1)[..., None]
    return vals.transpose(0, 1, 3, 2).reshape(g * 512, n)


E2M1 = np.array([0.0, 0.5, 1.0, 1.5, 2.0, 3.0, 4.0, 6.0, -0.0, -0.5, -1.0, -1.5, -2.0, -3.0, -4.0, -6.0])


def pack_fp4(w):
    k, n = w.shape
    w = f64(np.asarray(w, np.float32).astype(ml_dtypes.bfloat16)).reshape(k // 32, 32, n)
    amax = np.abs(w).max(1)
    mant, ex = np.frexp(amax / 6.0)
    byte = np.clip(np.where(amax > 0, np.where(mant > 0.5, ex, ex - 1) + 127, 1), 1, 254)
    scaled = (w * np.exp2(127.0 - byte)[:, None, :]).reshape(k, n).astype(np.float32)
    c = np.ascontiguousarray(scaled.reshape(k // 512, 128, 4, n).transpose(0, 1, 3, 2)).astype(ml_dtypes.float4_e2m1fn).view(np.uint8) & 0xF
    words = (c[..., 0::2] | (c[..., 1::2] << 4)).reshape(k // 512, 128, 2 * n)
    return np.ascontiguousarray(words), np.ascontiguousarray(byte.astype(np.uint8).reshape(k // 512, 16, n))


def unpack_fp4(words, scales):
    g, _, n = scales.shape
    words = np.ascontiguousarray(words).reshape(g, 128, n, 2)
    nib = np.empty((g, 128, n, 4), np.uint8)
    nib[..., 0::2] = words & 0xF
    nib[..., 1::2] = words >> 4
    vals = E2M1[nib] * np.repeat(np.exp2(scales.astype(np.float64) - 127.0), 8, axis=1)[..., None]
    return vals.transpose(0, 1, 3, 2).reshape(g * 512, n)


def planes(y):
    n, m = y.shape
    v = y.astype(np.float32).astype(ml_dtypes.bfloat16).astype(np.float64).reshape(n // 32, 32, m)
    top = np.abs(v).max(1)
    byte = np.clip(np.where(top > 0, np.frexp(top)[1] - 1 + 127 - 7, 1), 1, 254)
    codes = (v * np.exp2(127.0 - byte)[:, None, :]).reshape(n, m).astype(np.float32).astype(ml_dtypes.float8_e4m3fn).view(np.uint8)
    words = codes.reshape(n // 512, 128, 4, m).transpose(0, 1, 3, 2)
    return np.ascontiguousarray(words), np.ascontiguousarray(byte.astype(np.uint8).reshape(n // 512, 16, m))


K, T, S, N, H, U = 512, 2048, 512, 512, 512, 1024


def setup_inputs():
    n = np.random.standard_normal
    s = mx_kscale(K)[:, None]
    u = mx_kscale(H)
    packed_xT = pack_weight(n((K, T)) * s)
    packed_w1 = pack_fp4(n((K, N)) / np.sqrt(K) / s)
    packed_w2 = pack_fp4(n((H, N)) / np.sqrt(H) / u[:, None])
    return {
        "x_words": packed_xT[0],
        "x_scales": packed_xT[1],
        "w1_words": packed_w1[0],
        "w1_scales": packed_w1[1],
        "wa": (np.random.uniform(0.1, 0.45, (H, U))).astype(np.float32),
        "wb": (np.random.uniform(0.1, 0.45, (H, U))).astype(np.float32),
        "unit": (np.random.uniform(0.6, 1.4, (H, 1)) * u[:, None]).astype(np.float32),
        "w2_words": packed_w2[0],
        "w2_scales": packed_w2[1],
        "offs": striped(np.random.permutation(T)[:S]),
        "va": striped(np.random.permutation(np.concatenate([np.arange(S), np.random.randint(0, S, U - S)]))),
        "vb": striped(np.random.permutation(np.concatenate([np.arange(S), np.random.randint(0, S, U - S)]))),
        "vc": striped(np.random.permutation(np.concatenate([np.arange(S), np.random.randint(0, S, U - S)]))),
    }


def reference(x_words, x_scales, w1_words, w1_scales, wa, wb, unit, w2_words, w2_scales, offs, va, vb, vc):
    xq = unpack_weight(x_words, x_scales)[:, unstriped(offs)]
    y = unpack_fp4(w1_words, w1_scales).T @ xq
    ya = y[:, unstriped(va)]
    yb = y[:, unstriped(vb)]
    yvc = y[:, unstriped(vc)]
    fine = f64(wa) * ya + f64(wb) * yb + yvc * (-1.0 * (f64(wa) + f64(wb)) + 1.0)
    hid = f64(unit) * (fine + 0.4 * (np.maximum(np.maximum(ya, yb), yvc) - (np.minimum(np.minimum(ya, yb), yvc))))
    out_0 = unpack_fp4(w2_words, w2_scales).T @ mxq(hid, 0, "e4m3")
    return (out_0,) + planes(out_0)

@@ -1,0 +1,285 @@
+from contextlib import ExitStack
+
+import concourse.mybir as mybir
+from concourse.masks import make_identity
+
+K, T, S, N, H, U = 512, 2048, 512, 512, 512, 1024
+FLOPS = 2 * K * N * S + 2 * H * N * U
+
+F32 = mybir.dt.float32
+BF16 = mybir.dt.bfloat16
+I32 = mybir.dt.int32
+U32 = mybir.dt.uint32
+U16 = mybir.dt.uint16
+U8 = mybir.dt.uint8
+FP8X4 = mybir.dt.float8_e4m3fn_x4
+FP4X4 = mybir.dt.float4_e2m1fn_x4
+ALU = mybir.AluOpType
+ACT = mybir.ActivationFunctionType
+
+P = 128
+PACK = 4
+SPREAD = 0.4
+WIDTHS = (256, 256, 256, 128, 128)
+BYC, BYB, BT, BL = 2, 1, 2, 3
+RB = 2
+ORDER = "ga0 gb0 tn1 ba0 ta0 gc-1 hc1 db0 pr1 bb0 lg0 tb0 rs1 pl2"
+YV = (1, 2, 3)
+
+
+def load_scale_rows(queues, plane, rows):
+    for quad in range(4):
+        queues[quad].dma_start(
+            out=plane[32 * quad : 32 * quad + 4, :].bitcast(I32),
+            in_=rows[0, 4 * quad : 4 * quad + 4, :].bitcast(I32),
+        )
+
+
+def tile_picked_ybaryin_rng_po_kernel(
+    tc, x_words, x_scales, w1_words, w1_scales, wa, wb, unit, w2_words, w2_scales, offs, va, vb, vc, out_0, out_1, out_2
+):
+    nc = tc.nc
+    with ExitStack() as ctx:
+        keep = ctx.enter_context(tc.tile_pool(name="keep", bufs=1))
+        work = ctx.enter_context(tc.tile_pool(name="work", bufs=2))
+        late = ctx.enter_context(tc.tile_pool(name="late", bufs=3))
+        sums = ctx.enter_context(tc.psum_pool(name="sums", bufs=4))
+        small = ctx.enter_context(tc.psum_pool(name="small", bufs=2))
+
+        offs_t = keep.tile([P, S // 16], U16)
+        va_t = keep.tile([P, U // 16], U16)
+        vb_t = keep.tile([P, U // 16], U16)
+        vc_t = keep.tile([P, U // 16], U16)
+        x_tab = keep.tile([P, T], U32, align_bytes=64)
+        xs_tab = keep.tile([P, T], U8, align_bytes=64)
+        w1_t = keep.tile([P, 2 * N], U8, align_bytes=64)
+        w1s_t = keep.tile([P, N], U8, align_bytes=64)
+        w2_raw = keep.tile([P, 2 * N], U8, align_bytes=64)
+        w2s_raw = keep.tile([P, N], U8, align_bytes=64)
+        unit_t = keep.tile([P, PACK], F32)
+
+        nc.gpsimd.memset(xs_tab[:].bitcast(I32), 0)
+        nc.vector.memset(w1s_t[:].bitcast(I32), 0)
+        nc.vector.memset(w2s_raw[:].bitcast(I32), 0)
+
+        nc.sync.dma_start(offs_t[:], offs)
+        nc.sync.dma_start(vc_t[:], vc)
+        load_scale_rows([nc.sync] * 4, xs_tab, x_scales)
+        nc.sync.dma_start(out=x_tab[:].bitcast(I32), in_=x_words[0].rearrange("p c r -> p (c r)").bitcast(I32))
+        nc.sync.dma_start(out=w1_t[:].bitcast(I32), in_=w1_words[0].bitcast(I32))
+        load_scale_rows([nc.sync] * 4, w1s_t, w1_scales)
+        nc.sync.dma_start(va_t[:], va)
+        nc.sync.dma_start(vb_t[:], vb)
+        nc.sync.dma_start(out=w2_raw[:].bitcast(I32), in_=w2_words[0].bitcast(I32))
+        load_scale_rows([nc.sync] * 4, w2s_raw, w2_scales)
+        nc.sync.dma_start(out=unit_t[:], in_=unit.rearrange("(p j) o -> p (j o)", j=PACK))
+
+        wa_rows = wa.rearrange("(t p) r -> p t r", p=P)
+        wb_rows = wb.rearrange("(t p) r -> p t r", p=P)
+        wa_t, wb_t = [], []
+        start = 0
+        for n, width in enumerate(WIDTHS):
+            wa_t.append(keep.tile([P, PACK, width], F32, name=f"wa{n}"))
+            wb_t.append(keep.tile([P, PACK, width], F32, name=f"wb{n}"))
+            nc.sync.dma_start(out=wa_t[n][:], in_=wa_rows[:, :, start : start + width])
+            nc.sync.dma_start(out=wb_t[n][:], in_=wb_rows[:, :, start : start + width])
+            start += width
+
+        ident = keep.tile([P, P], F32)
+        make_identity(nc, ident[:])
+
+        xs_g = keep.tile([P, S], U8, align_bytes=64)
+        x_g = keep.tile([P, S], U32, align_bytes=64)
+        nc.vector.tensor_copy(xs_g[:], xs_tab[:].indirect(offs_t[:]))
+        nc.vector.tensor_copy(x_g[:], x_tab[:].indirect(offs_t[:]))
+
+        y = []
+        for t in range(PACK):
+            acc = sums.tile([P, S], F32, tag="sum", name="acc")
+            nc.tensor.matmul_mx(
+                out=acc[:],
+                lhsT=w1_t[:, 2 * P * t : 2 * P * (t + 1)].bitcast(FP4X4),
+                lhsT_scale=w1s_t[:, P * t : P * (t + 1)],
+                rhs=x_g[:].bitcast(FP8X4),
+                rhs_scale=xs_g[:],
+                start=True,
+                stop=True,
+            )
+            y.append(keep.tile([P, S], F32, name=f"y{t}"))
+            if t not in YV:
+                nc.scalar.copy(y[t][:], acc[:])
+            else:
+                nc.vector.tensor_copy(y[t][:], acc[:])
+
+        w2_t = keep.tile([P, PACK, P, 2], U8, align_bytes=64)
+        w2s_t = keep.tile([P, PACK, P], U8, align_bytes=64)
+        nc.gpsimd.tensor_copy(w2_t[:], w2_raw[:].rearrange("p (m t b) -> p t m b", t=PACK, b=2))
+        nc.gpsimd.tensor_copy(w2s_t[:], w2s_raw[:].rearrange("p (m t) -> p t m", t=PACK))
+
+        unit_ps = small.tile([P, PACK, P], F32, tag="res", name="unit_ps")
+        for j in range(PACK):
+            nc.tensor.transpose(unit_ps[:, j, :], unit_t[:, j : j + 1].to_broadcast([P, P]), ident[:])
+        unit_row = keep.tile([P, 2, P, 2], F32)
+        nc.scalar.copy(unit_row[:], unit_ps[:].rearrange("r (u e) p -> r u p e", e=2))
+
+        out_scales = keep.tile([P, U], U8, align_bytes=64)
+        out_rows = out_0.rearrange("(p t) r -> p t r", t=PACK)
+        out_words = out_1[0].rearrange("p c r -> p (c r)").bitcast(I32)
+
+        starts = [sum(WIDTHS[:n]) for n in range(len(WIDTHS))]
+        flat = "p t r -> p (t r)"
+        st = [dict() for n in WIDTHS]
+
+        def entries(n):
+            return slice(starts[n] // 16, (starts[n] + WIDTHS[n]) // 16)
+
+        def add_term(n, term):
+            st[n]["added"] = st[n].get("added", 0) + 1
+            for b, acc in enumerate(st[n]["acc"]):
+                for t in range(PACK):
+                    nc.tensor.matmul(
+                        acc[:, P * t : P * (t + 1)],
+                        term[:, t, P * b : P * (b + 1)],
+                        ident[:],
+                        start=(st[n]["added"] == 1 and t == 0),
+                        stop=(st[n]["added"] == 6 and t == PACK - 1),
+                        is_transpose=True,
+                    )
+
+        def gc(n):
+            yc = work.tile([P, PACK, WIDTHS[n]], F32, bufs=BYC)
+            for t in range(PACK):
+                nc.scalar.activation(yc[:, t, :], y[t][:].indirect(vc_t[:, entries(n)]), ACT.Copy)
+            st[n]["yc"] = yc
+
+        def ga(n):
+            da = work.tile([P, PACK, WIDTHS[n]], F32, bufs=BT)
+            yc = st[n]["yc"]
+            for t in range(PACK):
+                nc.vector.tensor_tensor(da[:, t, :], y[t][:].indirect(va_t[:, entries(n)]), yc[:, t, :], ALU.subtract)
+            st[n]["da"] = da
+            st[n]["acc"] = [sums.tile([P, S], F32, tag="sum", name="acc") for b in range(WIDTHS[n] // P)]
+            add_term(n, yc)
+
+        def gb(n):
+            yb4 = work.tile([P, PACK, WIDTHS[n]], F32, bufs=BYB)
+            for t in range(PACK):
+                nc.scalar.activation(yb4[:, t, :], y[t][:].indirect(vb_t[:, entries(n)]), ACT.Copy, scale=SPREAD)
+            st[n]["yb4"] = yb4
+
+        def ta(n):
+            term_a = work.tile([P, PACK, WIDTHS[n]], F32, bufs=BT)
+            nc.vector.tensor_tensor(term_a[:], st[n]["da"][:], wa_t[n][:], ALU.mult)
+            add_term(n, term_a)
+
+        def ba(n):
+            below_a = work.tile([P, PACK, WIDTHS[n]], F32, bufs=BT)
+            nc.scalar.activation(below_a[:], st[n]["da"][:], ACT.Relu, scale=-SPREAD)
+            add_term(n, below_a)
+
+        def db(n):
+            db4 = work.tile([P, PACK, WIDTHS[n]], F32, bufs=BT)
+            nc.vector.scalar_tensor_tensor(
+                db4[:].rearrange(flat), st[n]["yc"][:].rearrange(flat), -SPREAD, st[n]["yb4"][:].rearrange(flat), ALU.mult, ALU.add
+            )
+            st[n]["db4"] = db4
+
+        def lg(n):
+            larger = work.tile([P, PACK, WIDTHS[n]], F32, bufs=BT)
+            nc.vector.scalar_tensor_tensor(
+                larger[:].rearrange(flat), st[n]["da"][:].rearrange(flat), SPREAD, st[n]["db4"][:].rearrange(flat), ALU.mult, ALU.max
+            )
+            add_term(n, larger)
+
+        def tb(n):
+            term_b = work.tile([P, PACK, WIDTHS[n]], F32, bufs=BT)
+            nc.vector.scalar_tensor_tensor(
+                term_b[:].rearrange(flat), st[n]["db4"][:].rearrange(flat), 1.0 / SPREAD, wb_t[n][:].rearrange(flat), ALU.mult, ALU.mult
+            )
+            add_term(n, term_b)
+
+        def bb(n):
+            db4 = st[n]["db4"]
+            below_b = work.tile([P, PACK, WIDTHS[n]], F32, bufs=BT)
+            if RB > 0:
+                nc.scalar.activation(below_b[:, :RB, :], db4[:, :RB, :], ACT.Relu, scale=-1.0)
+            if RB < PACK:
+                nc.vector.tensor_scalar(below_b[:, RB:, :], db4[:, RB:, :], -1.0, 0.0, ALU.mult, ALU.max)
+            add_term(n, below_b)
+
+        def tn(n):
+            blocks = WIDTHS[n] // P
+            back = small.tile([P, blocks, 2, P], F32, tag="back", name="back")
+            for b in range(blocks):
+                acc = st[n]["acc"][b]
+                hid_t = late.tile([P, 2, P, 2], BF16, align_bytes=64, bufs=BL)
+                nc.vector.tensor_tensor(
+                    hid_t[:], acc[:].rearrange("r (p u e) -> r u p e", u=2, e=2), unit_row[:], ALU.mult
+                )
+                pairs = hid_t[:].rearrange("r u p e -> r (u p e)").bitcast(F32)
+                for u in range(2):
+                    nc.tensor.transpose(back[:, b, u, :], pairs[:, P * u : P * (u + 1)], ident[:])
+            st[n]["back"] = back
+
+        def hc(n):
+            hid = late.tile([P, WIDTHS[n] * PACK], BF16, align_bytes=64, bufs=BL)
+            nc.scalar.copy(
+                hid[:].bitcast(F32).rearrange("p (b r u) -> p b r u", b=WIDTHS[n] // P, u=2),
+                st[n]["back"][:].rearrange("p b u r -> p b r u"),
+            )
+            st[n]["hid"] = hid
+
+        def pr(n):
+            width = WIDTHS[n]
+            hid_codes = late.tile([P, width], U32, align_bytes=64, bufs=BL)
+            hid_scales = late.tile([P, width], U8, align_bytes=64, bufs=BL)
+            nc.vector.quantize_mx(out=hid_codes[:].bitcast(FP8X4), scales=hid_scales[:], in_=st[n]["hid"][:])
+            st[n]["res_ps"] = []
+            for b in range(width // P):
+                sub = slice(P * b, P * (b + 1))
+                res_ps = small.tile([P, PACK, P], F32, tag="res", name="res_ps")
+                for t in range(PACK):
+                    nc.tensor.matmul_mx(
+                        out=res_ps[:, t, :],
+                        lhsT=w2_t[:, t, :, :].rearrange("p m b -> p (m b)").bitcast(FP4X4),
+                        lhsT_scale=w2s_t[:, t, :],
+                        rhs=hid_codes[:, sub].bitcast(FP8X4),
+                        rhs_scale=hid_scales[:, sub],
+                        start=True,
+                        stop=True,
+                    )
+                st[n]["res_ps"].append(res_ps)
+
+        def rs(n):
+            width = WIDTHS[n]
+            cols = slice(starts[n], starts[n] + width)
+            res = late.tile([P, PACK, width], F32, bufs=BL)
+            res16 = late.tile([P, width, PACK], BF16, align_bytes=64, bufs=BL)
+            for b, res_ps in enumerate(st[n]["res_ps"]):
+                sub = slice(P * b, P * (b + 1))
+                nc.scalar.copy(res16[:, sub, :], res_ps[:].rearrange("p t r -> p r t"))
+                nc.scalar.copy(res[:, :, sub], res_ps[:])
+            nc.sync.dma_start(out=out_rows[:, :, cols], in_=res[:])
+            st[n]["res16"] = res16
+
+        def pl(n):
+            width = WIDTHS[n]
+            cols = slice(starts[n], starts[n] + width)
+            out_codes = late.tile([P, width], U32, align_bytes=64, bufs=BL)
+            nc.vector.quantize_mx(
+                out=out_codes[:].bitcast(FP8X4), scales=out_scales[:, cols], in_=st[n]["res16"][:].rearrange("p r t -> p (r t)")
+            )
+            nc.sync.dma_start(out=out_words[:, cols], in_=out_codes[:].bitcast(I32))
+
+        stage = dict(gc=gc, ga=ga, gb=gb, ta=ta, ba=ba, db=db, lg=lg, tb=tb, bb=bb, tn=tn, hc=hc, pr=pr, rs=rs, pl=pl)
+        for step in range(-2, len(WIDTHS) + 3):
+            for key in ORDER.split():
+                n = step - int(key[2:])
+                if 0 <= n < len(WIDTHS):
+                    stage[key[:2]](n)
+
+        for quad in range(4):
+            nc.sync.dma_start(
+                out=out_2[0, 4 * quad : 4 * quad + 4, :].bitcast(I32),
+                in_=out_scales[32 * quad : 32 * quad + 4, :].bitcast(I32),
+            )

@@ -21,9 +21,14 @@ P = 128
 PACK = 4
 SPREAD = 0.4
 WIDTHS = (256, 256, 256, 128, 128)
-BYC, BYB, BT, BL = 2, 1, 2, 3
-RB = 2
-ORDER = "ga0 gb0 tn1 ba0 ta0 gc-1 hc1 db0 pr1 bb0 lg0 tb0 rs1 pl2"
+BYC, BYB, BT, BL = 2, 2, 2, 3
+FUSED = (0,)
+FOUR = ()
+RAS = ()
+R16 = "V"
+HS = (2, 3, 4)
+RS = (0, 1, 2, 3, 4)
+ORDER = "gc-1 ga-1 gb-1 da0 sa0 db0 ra0 tn1 sb0 nn0 hc1 tt0 pr1 rs1 pl2"
 YV = (1, 2, 3)
 
 
@@ -63,30 +68,35 @@ def tile_picked_ybaryin_rng_po_kernel(
         nc.vector.memset(w2s_raw[:].bitcast(I32), 0)
 
         nc.sync.dma_start(offs_t[:], offs)
-        nc.sync.dma_start(vc_t[:], vc)
+        nc.sync.dma_start(out=unit_t[:], in_=unit.rearrange("(p j) o -> p (j o)", j=PACK))
         load_scale_rows([nc.sync] * 4, xs_tab, x_scales)
         nc.sync.dma_start(out=x_tab[:].bitcast(I32), in_=x_words[0].rearrange("p c r -> p (c r)").bitcast(I32))
         nc.sync.dma_start(out=w1_t[:].bitcast(I32), in_=w1_words[0].bitcast(I32))
         load_scale_rows([nc.sync] * 4, w1s_t, w1_scales)
+        nc.sync.dma_start(vc_t[:], vc)
         nc.sync.dma_start(va_t[:], va)
         nc.sync.dma_start(vb_t[:], vb)
         nc.sync.dma_start(out=w2_raw[:].bitcast(I32), in_=w2_words[0].bitcast(I32))
         load_scale_rows([nc.sync] * 4, w2s_raw, w2_scales)
-        nc.sync.dma_start(out=unit_t[:], in_=unit.rearrange("(p j) o -> p (j o)", j=PACK))
 
         wa_rows = wa.rearrange("(t p) r -> p t r", p=P)
         wb_rows = wb.rearrange("(t p) r -> p t r", p=P)
-        wa_t, wb_t = [], []
+        w_t = []
         start = 0
         for n, width in enumerate(WIDTHS):
-            wa_t.append(keep.tile([P, PACK, width], F32, name=f"wa{n}"))
-            wb_t.append(keep.tile([P, PACK, width], F32, name=f"wb{n}"))
-            nc.sync.dma_start(out=wa_t[n][:], in_=wa_rows[:, :, start : start + width])
-            nc.sync.dma_start(out=wb_t[n][:], in_=wb_rows[:, :, start : start + width])
+            w_t.append(keep.tile([P, 2, PACK, width], F32, name=f"w{n}"))
+            nc.sync.dma_start(out=w_t[n][:, 0], in_=wa_rows[:, :, start : start + width])
+            nc.sync.dma_start(out=w_t[n][:, 1], in_=wb_rows[:, :, start : start + width])
             start += width
 
         ident = keep.tile([P, P], F32)
         make_identity(nc, ident[:])
+
+        unit_ps = small.tile([P, PACK, P], F32, tag="res", name="unit_ps")
+        for j in range(PACK):
+            nc.tensor.transpose(unit_ps[:, j, :], unit_t[:, j : j + 1].to_broadcast([P, P]), ident[:])
+        unit_row = keep.tile([P, 2, P, 2], F32)
+        nc.vector.tensor_copy(unit_row[:], unit_ps[:].rearrange("r (u e) p -> r u p e", e=2))
 
         xs_g = keep.tile([P, S], U8, align_bytes=64)
         x_g = keep.tile([P, S], U32, align_bytes=64)
@@ -107,20 +117,14 @@ def tile_picked_ybaryin_rng_po_kernel(
             )
             y.append(keep.tile([P, S], F32, name=f"y{t}"))
             if t not in YV:
-                nc.scalar.copy(y[t][:], acc[:])
+                nc.scalar.activation(y[t][:], acc[:], ACT.Copy, scale=1.0)
             else:
-                nc.vector.tensor_copy(y[t][:], acc[:])
+                nc.vector.tensor_scalar(y[t][:], acc[:], 1.0, None, ALU.mult)
 
         w2_t = keep.tile([P, PACK, P, 2], U8, align_bytes=64)
         w2s_t = keep.tile([P, PACK, P], U8, align_bytes=64)
         nc.gpsimd.tensor_copy(w2_t[:], w2_raw[:].rearrange("p (m t b) -> p t m b", t=PACK, b=2))
         nc.gpsimd.tensor_copy(w2s_t[:], w2s_raw[:].rearrange("p (m t) -> p t m", t=PACK))
-
-        unit_ps = small.tile([P, PACK, P], F32, tag="res", name="unit_ps")
-        for j in range(PACK):
-            nc.tensor.transpose(unit_ps[:, j, :], unit_t[:, j : j + 1].to_broadcast([P, P]), ident[:])
-        unit_row = keep.tile([P, 2, P, 2], F32)
-        nc.scalar.copy(unit_row[:], unit_ps[:].rearrange("r (u e) p -> r u p e", e=2))
 
         out_scales = keep.tile([P, U], U8, align_bytes=64)
         out_rows = out_0.rearrange("(p t) r -> p t r", t=PACK)
@@ -128,6 +132,7 @@ def tile_picked_ybaryin_rng_po_kernel(
 
         starts = [sum(WIDTHS[:n]) for n in range(len(WIDTHS))]
         flat = "p t r -> p (t r)"
+        flat2 = "p l t r -> p (l t r)"
         st = [dict() for n in WIDTHS]
 
         def entries(n):
@@ -142,7 +147,7 @@ def tile_picked_ybaryin_rng_po_kernel(
                         term[:, t, P * b : P * (b + 1)],
                         ident[:],
                         start=(st[n]["added"] == 1 and t == 0),
-                        stop=(st[n]["added"] == 6 and t == PACK - 1),
+                        stop=(st[n]["added"] == (4 if n in FOUR else 5) and t == PACK - 1),
                         is_transpose=True,
                     )
 
@@ -153,13 +158,12 @@ def tile_picked_ybaryin_rng_po_kernel(
             st[n]["yc"] = yc
 
         def ga(n):
-            da = work.tile([P, PACK, WIDTHS[n]], F32, bufs=BT)
-            yc = st[n]["yc"]
+            if n in FUSED:
+                return
+            ya4 = work.tile([P, PACK, WIDTHS[n]], F32, bufs=BYB)
             for t in range(PACK):
-                nc.vector.tensor_tensor(da[:, t, :], y[t][:].indirect(va_t[:, entries(n)]), yc[:, t, :], ALU.subtract)
-            st[n]["da"] = da
-            st[n]["acc"] = [sums.tile([P, S], F32, tag="sum", name="acc") for b in range(WIDTHS[n] // P)]
-            add_term(n, yc)
+                nc.scalar.activation(ya4[:, t, :], y[t][:].indirect(va_t[:, entries(n)]), ACT.Copy, scale=SPREAD)
+            st[n]["ya4"] = ya4
 
         def gb(n):
             yb4 = work.tile([P, PACK, WIDTHS[n]], F32, bufs=BYB)
@@ -167,63 +171,90 @@ def tile_picked_ybaryin_rng_po_kernel(
                 nc.scalar.activation(yb4[:, t, :], y[t][:].indirect(vb_t[:, entries(n)]), ACT.Copy, scale=SPREAD)
             st[n]["yb4"] = yb4
 
-        def ta(n):
-            term_a = work.tile([P, PACK, WIDTHS[n]], F32, bufs=BT)
-            nc.vector.tensor_tensor(term_a[:], st[n]["da"][:], wa_t[n][:], ALU.mult)
-            add_term(n, term_a)
-
-        def ba(n):
-            below_a = work.tile([P, PACK, WIDTHS[n]], F32, bufs=BT)
-            nc.scalar.activation(below_a[:], st[n]["da"][:], ACT.Relu, scale=-SPREAD)
-            add_term(n, below_a)
+        def da(n):
+            diff_a = work.tile([P, PACK, WIDTHS[n]], F32, bufs=BT)
+            st[n]["da"] = diff_a
+            yc = st[n]["yc"]
+            if n in FUSED:
+                for t in range(PACK):
+                    nc.vector.tensor_tensor(diff_a[:, t, :], y[t][:].indirect(va_t[:, entries(n)]), yc[:, t, :], ALU.subtract)
+            else:
+                nc.vector.scalar_tensor_tensor(
+                    diff_a[:].rearrange(flat), yc[:].rearrange(flat), -SPREAD, st[n]["ya4"][:].rearrange(flat), ALU.mult, ALU.add
+                )
+            st[n]["ka"] = SPREAD if n in FUSED else 1.0
+            st[n]["acc"] = [sums.tile([P, S], F32, tag="sum", name="acc") for b in range(WIDTHS[n] // P)]
+            add_term(n, yc)
 
         def db(n):
-            db4 = work.tile([P, PACK, WIDTHS[n]], F32, bufs=BT)
+            diff_b = work.tile([P, PACK, WIDTHS[n]], F32, bufs=BT)
+            st[n]["db"] = diff_b
             nc.vector.scalar_tensor_tensor(
-                db4[:].rearrange(flat), st[n]["yc"][:].rearrange(flat), -SPREAD, st[n]["yb4"][:].rearrange(flat), ALU.mult, ALU.add
+                diff_b[:].rearrange(flat), st[n]["yc"][:].rearrange(flat), -SPREAD, st[n]["yb4"][:].rearrange(flat), ALU.mult, ALU.add
             )
-            st[n]["db4"] = db4
 
-        def lg(n):
-            larger = work.tile([P, PACK, WIDTHS[n]], F32, bufs=BT)
+        def sa(n):
+            term_a = work.tile([P, PACK, WIDTHS[n]], F32, bufs=BT)
             nc.vector.scalar_tensor_tensor(
-                larger[:].rearrange(flat), st[n]["da"][:].rearrange(flat), SPREAD, st[n]["db4"][:].rearrange(flat), ALU.mult, ALU.max
+                term_a[:].rearrange(flat), st[n]["da"][:].rearrange(flat), st[n]["ka"] / SPREAD, w_t[n][:, 0].rearrange(flat), ALU.mult, ALU.mult
             )
-            add_term(n, larger)
+            add_term(n, term_a)
 
-        def tb(n):
+        def sb(n):
             term_b = work.tile([P, PACK, WIDTHS[n]], F32, bufs=BT)
             nc.vector.scalar_tensor_tensor(
-                term_b[:].rearrange(flat), st[n]["db4"][:].rearrange(flat), 1.0 / SPREAD, wb_t[n][:].rearrange(flat), ALU.mult, ALU.mult
+                term_b[:].rearrange(flat), st[n]["db"][:].rearrange(flat), 1.0 / SPREAD, w_t[n][:, 1].rearrange(flat), ALU.mult, ALU.mult
             )
             add_term(n, term_b)
 
-        def bb(n):
-            db4 = st[n]["db4"]
-            below_b = work.tile([P, PACK, WIDTHS[n]], F32, bufs=BT)
-            if RB > 0:
-                nc.scalar.activation(below_b[:, :RB, :], db4[:, :RB, :], ACT.Relu, scale=-1.0)
-            if RB < PACK:
-                nc.vector.tensor_scalar(below_b[:, RB:, :], db4[:, RB:, :], -1.0, 0.0, ALU.mult, ALU.max)
-            add_term(n, below_b)
+        def ra(n):
+            if n in FOUR:
+                return
+            above_a = work.tile([P, PACK, WIDTHS[n]], F32, bufs=BT)
+            if n in RAS:
+                nc.scalar.activation(above_a[:], st[n]["da"][:], ACT.Relu, scale=st[n]["ka"])
+            else:
+                nc.vector.tensor_scalar(above_a[:], st[n]["da"][:], st[n]["ka"], 0.0, ALU.mult, ALU.max)
+            add_term(n, above_a)
+
+        def nn(n):
+            least = work.tile([P, PACK, WIDTHS[n]], F32, bufs=BT)
+            nc.vector.scalar_tensor_tensor(
+                least[:].rearrange(flat), st[n]["da"][:].rearrange(flat), st[n]["ka"], st[n]["db"][:].rearrange(flat), ALU.mult, ALU.min
+            )
+            st[n]["least"] = least
+
+        def tt(n):
+            part = work.tile([P, PACK, WIDTHS[n]], F32, bufs=BT)
+            nc.vector.scalar_tensor_tensor(
+                part[:].rearrange(flat), st[n]["db"][:].rearrange(flat), 0.0, st[n]["least"][:].rearrange(flat), ALU.max, ALU.subtract
+            )
+            if n in FOUR:
+                above_a = work.tile([P, PACK, WIDTHS[n]], F32, bufs=BT)
+                nc.vector.scalar_tensor_tensor(
+                    above_a[:].rearrange(flat), st[n]["da"][:].rearrange(flat), 0.0, part[:].rearrange(flat), ALU.max, ALU.add
+                )
+                part = above_a
+            add_term(n, part)
+
+        def turn(n, b):
+            acc = st[n]["acc"][b]
+            hid_t = late.tile([P, 2, P, 2], BF16, align_bytes=64, bufs=BL)
+            nc.vector.tensor_tensor(
+                hid_t[:], acc[:].rearrange("r (p u e) -> r u p e", u=2, e=2), unit_row[:], ALU.mult
+            )
+            pairs = hid_t[:].rearrange("r u p e -> r (u p e)").bitcast(F32)
+            for u in range(2):
+                nc.tensor.transpose(st[n]["back"][:, b, u, :], pairs[:, P * u : P * (u + 1)], ident[:])
 
         def tn(n):
-            blocks = WIDTHS[n] // P
-            back = small.tile([P, blocks, 2, P], F32, tag="back", name="back")
-            for b in range(blocks):
-                acc = st[n]["acc"][b]
-                hid_t = late.tile([P, 2, P, 2], BF16, align_bytes=64, bufs=BL)
-                nc.vector.tensor_tensor(
-                    hid_t[:], acc[:].rearrange("r (p u e) -> r u p e", u=2, e=2), unit_row[:], ALU.mult
-                )
-                pairs = hid_t[:].rearrange("r u p e -> r (u p e)").bitcast(F32)
-                for u in range(2):
-                    nc.tensor.transpose(back[:, b, u, :], pairs[:, P * u : P * (u + 1)], ident[:])
-            st[n]["back"] = back
+            st[n]["back"] = small.tile([P, WIDTHS[n] // P, 2, P], F32, tag="back", name="back")
+            for b in range(WIDTHS[n] // P):
+                turn(n, b)
 
         def hc(n):
             hid = late.tile([P, WIDTHS[n] * PACK], BF16, align_bytes=64, bufs=BL)
-            nc.scalar.copy(
+            (nc.scalar.copy if n in HS else nc.vector.tensor_copy)(
                 hid[:].bitcast(F32).rearrange("p (b r u) -> p b r u", b=WIDTHS[n] // P, u=2),
                 st[n]["back"][:].rearrange("p b u r -> p b r u"),
             )
@@ -257,22 +288,26 @@ def tile_picked_ybaryin_rng_po_kernel(
             res16 = late.tile([P, width, PACK], BF16, align_bytes=64, bufs=BL)
             for b, res_ps in enumerate(st[n]["res_ps"]):
                 sub = slice(P * b, P * (b + 1))
-                nc.scalar.copy(res16[:, sub, :], res_ps[:].rearrange("p t r -> p r t"))
+                if R16 == "S" or n in RS:
+                    nc.scalar.copy(res16[:, sub, :], res_ps[:].rearrange("p t r -> p r t"))
                 nc.scalar.copy(res[:, :, sub], res_ps[:])
             nc.sync.dma_start(out=out_rows[:, :, cols], in_=res[:])
             st[n]["res16"] = res16
+            st[n]["res"] = res
 
         def pl(n):
             width = WIDTHS[n]
             cols = slice(starts[n], starts[n] + width)
+            if not (R16 == "S" or n in RS):
+                nc.vector.tensor_copy(st[n]["res16"][:], st[n]["res"][:].rearrange("p t r -> p r t"))
             out_codes = late.tile([P, width], U32, align_bytes=64, bufs=BL)
             nc.vector.quantize_mx(
                 out=out_codes[:].bitcast(FP8X4), scales=out_scales[:, cols], in_=st[n]["res16"][:].rearrange("p r t -> p (r t)")
             )
             nc.sync.dma_start(out=out_words[:, cols], in_=out_codes[:].bitcast(I32))
 
-        stage = dict(gc=gc, ga=ga, gb=gb, ta=ta, ba=ba, db=db, lg=lg, tb=tb, bb=bb, tn=tn, hc=hc, pr=pr, rs=rs, pl=pl)
-        for step in range(-2, len(WIDTHS) + 3):
+        stage = dict(gc=gc, ga=ga, gb=gb, da=da, db=db, sa=sa, sb=sb, ra=ra, nn=nn, tt=tt, tn=tn, hc=hc, pr=pr, rs=rs, pl=pl)
+        for step in range(-2, len(WIDTHS) + 5):
             for key in ORDER.split():
                 n = step - int(key[2:])
                 if 0 <= n < len(WIDTHS):

@@ -24,11 +24,16 @@ WIDTHS = (256, 256, 256, 128, 128)
 BYC, BYB, BT, BL = 2, 2, 2, 3
 FUSED = (0,)
 FOUR = ()
-RAS = ()
+SIX = ()
+RBS = ()
+RAS = (2, 3)
 R16 = "V"
-HS = (2, 3, 4)
+HS = (2, 3)
 RS = (0, 1, 2, 3, 4)
-ORDER = "gc-1 ga-1 gb-1 da0 sa0 db0 ra0 tn1 sb0 nn0 hc1 tt0 pr1 rs1 pl2"
+ORDER = "gc-1 ga-1 gb-1 da0 sa0 db0 ra0 tn1 sb0 nn0 hc1 tt0 rx0 pr1 rs1 pl2"
+LAST = "gc-1 ga-1 gb-1 da0 sa0 db0 ra0 sb0 nn0 tt0 rx0 tn1 hc1 pr1 rs1 pl2"
+NL = 2
+XH = 2
 YV = (1, 2, 3)
 
 
@@ -69,6 +74,7 @@ def tile_picked_ybaryin_rng_po_kernel(
 
         nc.sync.dma_start(offs_t[:], offs)
         nc.sync.dma_start(out=unit_t[:], in_=unit.rearrange("(p j) o -> p (j o)", j=PACK))
+        nc.sync.dma_start(out=w2_raw[:].bitcast(I32), in_=w2_words[0].bitcast(I32))
         load_scale_rows([nc.sync] * 4, xs_tab, x_scales)
         nc.sync.dma_start(out=x_tab[:].bitcast(I32), in_=x_words[0].rearrange("p c r -> p (c r)").bitcast(I32))
         nc.sync.dma_start(out=w1_t[:].bitcast(I32), in_=w1_words[0].bitcast(I32))
@@ -76,8 +82,6 @@ def tile_picked_ybaryin_rng_po_kernel(
         nc.sync.dma_start(vc_t[:], vc)
         nc.sync.dma_start(va_t[:], va)
         nc.sync.dma_start(vb_t[:], vb)
-        nc.sync.dma_start(out=w2_raw[:].bitcast(I32), in_=w2_words[0].bitcast(I32))
-        load_scale_rows([nc.sync] * 4, w2s_raw, w2_scales)
 
         wa_rows = wa.rearrange("(t p) r -> p t r", p=P)
         wb_rows = wb.rearrange("(t p) r -> p t r", p=P)
@@ -88,6 +92,8 @@ def tile_picked_ybaryin_rng_po_kernel(
             nc.sync.dma_start(out=w_t[n][:, 0], in_=wa_rows[:, :, start : start + width])
             nc.sync.dma_start(out=w_t[n][:, 1], in_=wb_rows[:, :, start : start + width])
             start += width
+            if n == 0:
+                load_scale_rows([nc.sync] * 4, w2s_raw, w2_scales)
 
         ident = keep.tile([P, P], F32)
         make_identity(nc, ident[:])
@@ -96,25 +102,28 @@ def tile_picked_ybaryin_rng_po_kernel(
         for j in range(PACK):
             nc.tensor.transpose(unit_ps[:, j, :], unit_t[:, j : j + 1].to_broadcast([P, P]), ident[:])
         unit_row = keep.tile([P, 2, P, 2], F32)
-        nc.vector.tensor_copy(unit_row[:], unit_ps[:].rearrange("r (u e) p -> r u p e", e=2))
+        nc.scalar.copy(unit_row[:], unit_ps[:].rearrange("r (u e) p -> r u p e", e=2))
 
         xs_g = keep.tile([P, S], U8, align_bytes=64)
         x_g = keep.tile([P, S], U32, align_bytes=64)
         nc.vector.tensor_copy(xs_g[:], xs_tab[:].indirect(offs_t[:]))
-        nc.vector.tensor_copy(x_g[:], x_tab[:].indirect(offs_t[:]))
+        half = S // XH
+        for h in range(XH):
+            nc.vector.tensor_copy(x_g[:, half * h : half * (h + 1)], x_tab[:].indirect(offs_t[:, half // 16 * h : half // 16 * (h + 1)]))
 
         y = []
         for t in range(PACK):
             acc = sums.tile([P, S], F32, tag="sum", name="acc")
-            nc.tensor.matmul_mx(
-                out=acc[:],
-                lhsT=w1_t[:, 2 * P * t : 2 * P * (t + 1)].bitcast(FP4X4),
-                lhsT_scale=w1s_t[:, P * t : P * (t + 1)],
-                rhs=x_g[:].bitcast(FP8X4),
-                rhs_scale=xs_g[:],
-                start=True,
-                stop=True,
-            )
+            for h in range(XH):
+                nc.tensor.matmul_mx(
+                    out=acc[:, half * h : half * (h + 1)],
+                    lhsT=w1_t[:, 2 * P * t : 2 * P * (t + 1)].bitcast(FP4X4),
+                    lhsT_scale=w1s_t[:, P * t : P * (t + 1)],
+                    rhs=x_g[:, half * h : half * (h + 1)].bitcast(FP8X4),
+                    rhs_scale=xs_g[:, half * h : half * (h + 1)],
+                    start=True,
+                    stop=True,
+                )
             y.append(keep.tile([P, S], F32, name=f"y{t}"))
             if t not in YV:
                 nc.scalar.activation(y[t][:], acc[:], ACT.Copy, scale=1.0)
@@ -123,8 +132,8 @@ def tile_picked_ybaryin_rng_po_kernel(
 
         w2_t = keep.tile([P, PACK, P, 2], U8, align_bytes=64)
         w2s_t = keep.tile([P, PACK, P], U8, align_bytes=64)
-        nc.gpsimd.tensor_copy(w2_t[:], w2_raw[:].rearrange("p (m t b) -> p t m b", t=PACK, b=2))
-        nc.gpsimd.tensor_copy(w2s_t[:], w2s_raw[:].rearrange("p (m t) -> p t m", t=PACK))
+        nc.vector.tensor_copy(w2_t[:], w2_raw[:].rearrange("p (m t b) -> p t m b", t=PACK, b=2))
+        nc.vector.tensor_copy(w2s_t[:], w2s_raw[:].rearrange("p (m t) -> p t m", t=PACK))
 
         out_scales = keep.tile([P, U], U8, align_bytes=64)
         out_rows = out_0.rearrange("(p t) r -> p t r", t=PACK)
@@ -147,7 +156,7 @@ def tile_picked_ybaryin_rng_po_kernel(
                         term[:, t, P * b : P * (b + 1)],
                         ident[:],
                         start=(st[n]["added"] == 1 and t == 0),
-                        stop=(st[n]["added"] == (4 if n in FOUR else 5) and t == PACK - 1),
+                        stop=(st[n]["added"] == (4 if n in FOUR else 6 if n in SIX else 5) and t == PACK - 1),
                         is_transpose=True,
                     )
 
@@ -184,7 +193,6 @@ def tile_picked_ybaryin_rng_po_kernel(
                 )
             st[n]["ka"] = SPREAD if n in FUSED else 1.0
             st[n]["acc"] = [sums.tile([P, S], F32, tag="sum", name="acc") for b in range(WIDTHS[n] // P)]
-            add_term(n, yc)
 
         def db(n):
             diff_b = work.tile([P, PACK, WIDTHS[n]], F32, bufs=BT)
@@ -199,6 +207,7 @@ def tile_picked_ybaryin_rng_po_kernel(
                 term_a[:].rearrange(flat), st[n]["da"][:].rearrange(flat), st[n]["ka"] / SPREAD, w_t[n][:, 0].rearrange(flat), ALU.mult, ALU.mult
             )
             add_term(n, term_a)
+            add_term(n, st[n]["yc"])
 
         def sb(n):
             term_b = work.tile([P, PACK, WIDTHS[n]], F32, bufs=BT)
@@ -212,20 +221,39 @@ def tile_picked_ybaryin_rng_po_kernel(
                 return
             above_a = work.tile([P, PACK, WIDTHS[n]], F32, bufs=BT)
             if n in RAS:
-                nc.scalar.activation(above_a[:], st[n]["da"][:], ACT.Relu, scale=st[n]["ka"])
+                nc.scalar.activation(above_a[:], st[n]["da"][:], ACT.Relu, scale=st[n]["ka"] * (-1.0 if n in SIX else 1.0))
             else:
-                nc.vector.tensor_scalar(above_a[:], st[n]["da"][:], st[n]["ka"], 0.0, ALU.mult, ALU.max)
-            add_term(n, above_a)
+                nc.vector.tensor_scalar(above_a[:], st[n]["da"][:], st[n]["ka"] * (-1.0 if n in SIX else 1.0), 0.0, ALU.mult, ALU.max)
+            st[n]["above_a"] = above_a
+            if n not in RAS:
+                add_term(n, above_a)
+
+        def rx(n):
+            if n in RAS and n not in FOUR:
+                add_term(n, st[n]["above_a"])
+            if n in RBS and n in SIX:
+                add_term(n, st[n]["part"])
 
         def nn(n):
             least = work.tile([P, PACK, WIDTHS[n]], F32, bufs=BT)
             nc.vector.scalar_tensor_tensor(
-                least[:].rearrange(flat), st[n]["da"][:].rearrange(flat), st[n]["ka"], st[n]["db"][:].rearrange(flat), ALU.mult, ALU.min
+                least[:].rearrange(flat), st[n]["da"][:].rearrange(flat), st[n]["ka"], st[n]["db"][:].rearrange(flat), ALU.mult, ALU.max if n in SIX else ALU.min
             )
             st[n]["least"] = least
+            if n in SIX:
+                add_term(n, least)
 
         def tt(n):
             part = work.tile([P, PACK, WIDTHS[n]], F32, bufs=BT)
+            if n in SIX:
+                if n in RBS:
+                    nc.scalar.activation(part[:], st[n]["db"][:], ACT.Relu, scale=-1.0)
+                else:
+                    nc.vector.tensor_scalar(part[:], st[n]["db"][:], -1.0, 0.0, ALU.mult, ALU.max)
+                st[n]["part"] = part
+                if n not in RBS:
+                    add_term(n, part)
+                return
             nc.vector.scalar_tensor_tensor(
                 part[:].rearrange(flat), st[n]["db"][:].rearrange(flat), 0.0, st[n]["least"][:].rearrange(flat), ALU.max, ALU.subtract
             )
@@ -306,15 +334,15 @@ def tile_picked_ybaryin_rng_po_kernel(
             )
             nc.sync.dma_start(out=out_words[:, cols], in_=out_codes[:].bitcast(I32))
 
-        stage = dict(gc=gc, ga=ga, gb=gb, da=da, db=db, sa=sa, sb=sb, ra=ra, nn=nn, tt=tt, tn=tn, hc=hc, pr=pr, rs=rs, pl=pl)
+        stage = dict(rx=rx, gc=gc, ga=ga, gb=gb, da=da, db=db, sa=sa, sb=sb, ra=ra, nn=nn, tt=tt, tn=tn, hc=hc, pr=pr, rs=rs, pl=pl)
         for step in range(-2, len(WIDTHS) + 5):
-            for key in ORDER.split():
+            for key in (LAST if step >= len(WIDTHS) - NL else ORDER).split():
                 n = step - int(key[2:])
                 if 0 <= n < len(WIDTHS):
                     stage[key[:2]](n)
 
         for quad in range(4):
-            nc.sync.dma_start(
+            (nc.sync if quad % 2 else nc.scalar).dma_start(
                 out=out_2[0, 4 * quad : 4 * quad + 4, :].bitcast(I32),
                 in_=out_scales[32 * quad : 32 * quad + 4, :].bitcast(I32),
             )

@@ -19,28 +19,25 @@ ACT = mybir.ActivationFunctionType
 
 P = 128
 PACK = 4
+LIST_ROWS = 16
 SPREAD = 0.4
-WIDTHS = (256, 256, 256, 128, 128)
-BYC, BYB, BT, BL = 2, 2, 2, 3
-FUSED = (0,)
-FOUR = ()
-SIX = ()
-RBS = ()
-RAS = (2, 3)
-R16 = "V"
-HS = (2, 3)
-RS = (0, 1, 2, 3, 4)
-ORDER = "gc-1 ga-1 gb-1 da0 sa0 db0 ra0 tn1 sb0 nn0 hc1 tt0 rx0 pr1 rs1 pl2"
-LAST = "gc-1 ga-1 gb-1 da0 sa0 db0 ra0 sb0 nn0 tt0 rx0 tn1 hc1 pr1 rs1 pl2"
-NL = 2
-XH = 2
-YV = (1, 2, 3)
+FLAT = "p t r -> p (t r)"
+
+WIDE, NARROW = 2 * P, P
+WIDTHS = (WIDE, WIDE, WIDE, NARROW, NARROW)
+CHUNKS = len(WIDTHS)
+STARTS = tuple(sum(WIDTHS[:n]) for n in range(CHUNKS))
+VECTOR_GATHERS_A_BELOW = 2
+SCALAR_RELU_FROM = 1
+SCALAR_WORD_COPY_FROM = 2
+SCALAR_COPIES_Y_BELOW = 2
+PLANES_LAG = 3
 
 
-def load_scale_rows(queues, plane, rows):
+def load_scale_rows(nc, scale_tile, rows):
     for quad in range(4):
-        queues[quad].dma_start(
-            out=plane[32 * quad : 32 * quad + 4, :].bitcast(I32),
+        nc.sync.dma_start(
+            out=scale_tile[32 * quad : 32 * quad + 4, :].bitcast(I32),
             in_=rows[0, 4 * quad : 4 * quad + 4, :].bitcast(I32),
         )
 
@@ -52,14 +49,14 @@ def tile_picked_ybaryin_rng_po_kernel(
     with ExitStack() as ctx:
         keep = ctx.enter_context(tc.tile_pool(name="keep", bufs=1))
         work = ctx.enter_context(tc.tile_pool(name="work", bufs=2))
-        late = ctx.enter_context(tc.tile_pool(name="late", bufs=3))
+        late = ctx.enter_context(tc.tile_pool(name="late", bufs=PLANES_LAG + 1))
         sums = ctx.enter_context(tc.psum_pool(name="sums", bufs=4))
         small = ctx.enter_context(tc.psum_pool(name="small", bufs=2))
 
-        offs_t = keep.tile([P, S // 16], U16)
-        va_t = keep.tile([P, U // 16], U16)
-        vb_t = keep.tile([P, U // 16], U16)
-        vc_t = keep.tile([P, U // 16], U16)
+        offs_t = keep.tile([P, S // LIST_ROWS], U16)
+        va_t = keep.tile([P, U // LIST_ROWS], U16)
+        vb_t = keep.tile([P, U // LIST_ROWS], U16)
+        vc_t = keep.tile([P, U // LIST_ROWS], U16)
         x_tab = keep.tile([P, T], U32, align_bytes=64)
         xs_tab = keep.tile([P, T], U8, align_bytes=64)
         w1_t = keep.tile([P, 2 * N], U8, align_bytes=64)
@@ -75,25 +72,24 @@ def tile_picked_ybaryin_rng_po_kernel(
         nc.sync.dma_start(offs_t[:], offs)
         nc.sync.dma_start(out=unit_t[:], in_=unit.rearrange("(p j) o -> p (j o)", j=PACK))
         nc.sync.dma_start(out=w2_raw[:].bitcast(I32), in_=w2_words[0].bitcast(I32))
-        load_scale_rows([nc.sync] * 4, xs_tab, x_scales)
+        load_scale_rows(nc, xs_tab, x_scales)
         nc.sync.dma_start(out=x_tab[:].bitcast(I32), in_=x_words[0].rearrange("p c r -> p (c r)").bitcast(I32))
         nc.sync.dma_start(out=w1_t[:].bitcast(I32), in_=w1_words[0].bitcast(I32))
-        load_scale_rows([nc.sync] * 4, w1s_t, w1_scales)
+        load_scale_rows(nc, w1s_t, w1_scales)
         nc.sync.dma_start(vc_t[:], vc)
         nc.sync.dma_start(va_t[:], va)
         nc.sync.dma_start(vb_t[:], vb)
 
         wa_rows = wa.rearrange("(t p) r -> p t r", p=P)
         wb_rows = wb.rearrange("(t p) r -> p t r", p=P)
-        w_t = []
-        start = 0
-        for n, width in enumerate(WIDTHS):
-            w_t.append(keep.tile([P, 2, PACK, width], F32, name=f"w{n}"))
-            nc.sync.dma_start(out=w_t[n][:, 0], in_=wa_rows[:, :, start : start + width])
-            nc.sync.dma_start(out=w_t[n][:, 1], in_=wb_rows[:, :, start : start + width])
-            start += width
+        weights = []
+        for n in range(CHUNKS):
+            cols = slice(STARTS[n], STARTS[n] + WIDTHS[n])
+            weights.append(keep.tile([P, 2, PACK, WIDTHS[n]], F32, name=f"weights{n}"))
+            nc.sync.dma_start(out=weights[n][:, 0], in_=wa_rows[:, :, cols])
+            nc.sync.dma_start(out=weights[n][:, 1], in_=wb_rows[:, :, cols])
             if n == 0:
-                load_scale_rows([nc.sync] * 4, w2s_raw, w2_scales)
+                load_scale_rows(nc, w2s_raw, w2_scales)
 
         ident = keep.tile([P, P], F32)
         make_identity(nc, ident[:])
@@ -107,242 +103,199 @@ def tile_picked_ybaryin_rng_po_kernel(
         xs_g = keep.tile([P, S], U8, align_bytes=64)
         x_g = keep.tile([P, S], U32, align_bytes=64)
         nc.vector.tensor_copy(xs_g[:], xs_tab[:].indirect(offs_t[:]))
-        half = S // XH
-        for h in range(XH):
-            nc.vector.tensor_copy(x_g[:, half * h : half * (h + 1)], x_tab[:].indirect(offs_t[:, half // 16 * h : half // 16 * (h + 1)]))
+        half = S // 2
+        halves = [slice(0, half), slice(half, S)]
+        for picked in halves:
+            offsets = offs_t[:, picked.start // LIST_ROWS : picked.stop // LIST_ROWS]
+            nc.vector.tensor_copy(x_g[:, picked], x_tab[:].indirect(offsets))
 
         y = []
         for t in range(PACK):
-            acc = sums.tile([P, S], F32, tag="sum", name="acc")
-            for h in range(XH):
+            y_ps = sums.tile([P, S], F32, tag="sum", name="y_ps")
+            for picked in halves:
                 nc.tensor.matmul_mx(
-                    out=acc[:, half * h : half * (h + 1)],
+                    out=y_ps[:, picked],
                     lhsT=w1_t[:, 2 * P * t : 2 * P * (t + 1)].bitcast(FP4X4),
                     lhsT_scale=w1s_t[:, P * t : P * (t + 1)],
-                    rhs=x_g[:, half * h : half * (h + 1)].bitcast(FP8X4),
-                    rhs_scale=xs_g[:, half * h : half * (h + 1)],
+                    rhs=x_g[:, picked].bitcast(FP8X4),
+                    rhs_scale=xs_g[:, picked],
                     start=True,
                     stop=True,
                 )
             y.append(keep.tile([P, S], F32, name=f"y{t}"))
-            if t not in YV:
-                nc.scalar.activation(y[t][:], acc[:], ACT.Copy, scale=1.0)
+            if t < SCALAR_COPIES_Y_BELOW:
+                nc.scalar.copy(y[t][:], y_ps[:])
             else:
-                nc.vector.tensor_scalar(y[t][:], acc[:], 1.0, None, ALU.mult)
+                nc.vector.tensor_copy(y[t][:], y_ps[:])
 
         w2_t = keep.tile([P, PACK, P, 2], U8, align_bytes=64)
         w2s_t = keep.tile([P, PACK, P], U8, align_bytes=64)
-        nc.vector.tensor_copy(w2_t[:], w2_raw[:].rearrange("p (m t b) -> p t m b", t=PACK, b=2))
-        nc.vector.tensor_copy(w2s_t[:], w2s_raw[:].rearrange("p (m t) -> p t m", t=PACK))
+        nc.vector.tensor_copy(w2_t[:], w2_raw[:].rearrange("p (c t b) -> p t c b", t=PACK, b=2))
+        nc.vector.tensor_copy(w2s_t[:], w2s_raw[:].rearrange("p (c t) -> p t c", t=PACK))
 
         out_scales = keep.tile([P, U], U8, align_bytes=64)
         out_rows = out_0.rearrange("(p t) r -> p t r", t=PACK)
         out_words = out_1[0].rearrange("p c r -> p (c r)").bitcast(I32)
 
-        starts = [sum(WIDTHS[:n]) for n in range(len(WIDTHS))]
-        flat = "p t r -> p (t r)"
-        flat2 = "p l t r -> p (l t r)"
-        st = [dict() for n in WIDTHS]
+        held = [{} for n in range(CHUNKS)]
 
-        def entries(n):
-            return slice(starts[n] // 16, (starts[n] + WIDTHS[n]) // 16)
+        def chunk_tile(n, name):
+            held[n][name] = work.tile([P, PACK, WIDTHS[n]], F32, name=name)
+            return held[n][name]
 
-        def add_term(n, term):
-            st[n]["added"] = st[n].get("added", 0) + 1
-            for b, acc in enumerate(st[n]["acc"]):
+        def looked_up(n, t, list_tile):
+            return y[t][:].indirect(list_tile[:, STARTS[n] // LIST_ROWS : (STARTS[n] + WIDTHS[n]) // LIST_ROWS])
+
+        def two_ops(out, in0, scalar, in1, op0, op1):
+            nc.vector.scalar_tensor_tensor(
+                out[:].rearrange(FLAT), in0[:].rearrange(FLAT), scalar, in1[:].rearrange(FLAT), op0, op1
+            )
+
+        def six_terms(n):
+            return WIDTHS[n] == WIDE
+
+        def relu_a_on_scalar(n):
+            return SCALAR_RELU_FROM <= n < CHUNKS - 1
+
+        def add_term(n, term, first=False, last=False):
+            for b, bank in enumerate(held[n]["banks"]):
                 for t in range(PACK):
                     nc.tensor.matmul(
-                        acc[:, P * t : P * (t + 1)],
+                        bank[:, P * t : P * (t + 1)],
                         term[:, t, P * b : P * (b + 1)],
                         ident[:],
-                        start=(st[n]["added"] == 1 and t == 0),
-                        stop=(st[n]["added"] == (4 if n in FOUR else 6 if n in SIX else 5) and t == PACK - 1),
+                        start=(first and t == 0),
+                        stop=(last and t == PACK - 1),
                         is_transpose=True,
                     )
 
-        def gc(n):
-            yc = work.tile([P, PACK, WIDTHS[n]], F32, bufs=BYC)
-            for t in range(PACK):
-                nc.scalar.activation(yc[:, t, :], y[t][:].indirect(vc_t[:, entries(n)]), ACT.Copy)
-            st[n]["yc"] = yc
-
-        def ga(n):
-            if n in FUSED:
-                return
-            ya4 = work.tile([P, PACK, WIDTHS[n]], F32, bufs=BYB)
-            for t in range(PACK):
-                nc.scalar.activation(ya4[:, t, :], y[t][:].indirect(va_t[:, entries(n)]), ACT.Copy, scale=SPREAD)
-            st[n]["ya4"] = ya4
-
-        def gb(n):
-            yb4 = work.tile([P, PACK, WIDTHS[n]], F32, bufs=BYB)
-            for t in range(PACK):
-                nc.scalar.activation(yb4[:, t, :], y[t][:].indirect(vb_t[:, entries(n)]), ACT.Copy, scale=SPREAD)
-            st[n]["yb4"] = yb4
-
-        def da(n):
-            diff_a = work.tile([P, PACK, WIDTHS[n]], F32, bufs=BT)
-            st[n]["da"] = diff_a
-            yc = st[n]["yc"]
-            if n in FUSED:
+        def scalar_gathers(n):
+            wanted = [("yc", vc_t, 1.0), ("ya4", va_t, SPREAD), ("yb4", vb_t, SPREAD)]
+            for name, list_tile, factor in wanted:
+                if name == "ya4" and n < VECTOR_GATHERS_A_BELOW:
+                    continue
+                corner = chunk_tile(n, name)
                 for t in range(PACK):
-                    nc.vector.tensor_tensor(diff_a[:, t, :], y[t][:].indirect(va_t[:, entries(n)]), yc[:, t, :], ALU.subtract)
+                    nc.scalar.activation(corner[:, t, :], looked_up(n, t, list_tile), ACT.Copy, scale=factor)
+
+        def first_terms(n):
+            yc = held[n]["yc"]
+            diff_a = chunk_tile(n, "diff_a")
+            if n < VECTOR_GATHERS_A_BELOW:
+                for t in range(PACK):
+                    nc.vector.tensor_tensor(diff_a[:, t, :], looked_up(n, t, va_t), yc[:, t, :], ALU.subtract)
+                to_a = SPREAD
             else:
-                nc.vector.scalar_tensor_tensor(
-                    diff_a[:].rearrange(flat), yc[:].rearrange(flat), -SPREAD, st[n]["ya4"][:].rearrange(flat), ALU.mult, ALU.add
-                )
-            st[n]["ka"] = SPREAD if n in FUSED else 1.0
-            st[n]["acc"] = [sums.tile([P, S], F32, tag="sum", name="acc") for b in range(WIDTHS[n] // P)]
+                two_ops(diff_a, yc, -SPREAD, held[n]["ya4"], ALU.mult, ALU.add)
+                to_a = 1.0
+            held[n]["to_a"] = to_a
+            held[n]["banks"] = [sums.tile([P, H], F32, tag="sum", name="bank") for b in range(WIDTHS[n] // P)]
+            term_a = chunk_tile(n, "term_a")
+            two_ops(term_a, diff_a, to_a / SPREAD, weights[n][:, 0], ALU.mult, ALU.mult)
+            add_term(n, term_a, first=True)
+            add_term(n, yc)
+            two_ops(chunk_tile(n, "diff_b"), yc, -SPREAD, held[n]["yb4"], ALU.mult, ALU.add)
+            relu_a = chunk_tile(n, "relu_a")
+            factor = -to_a if six_terms(n) else to_a
+            if relu_a_on_scalar(n):
+                nc.scalar.activation(relu_a[:], diff_a[:], ACT.Relu, scale=factor)
+            else:
+                nc.vector.tensor_scalar(relu_a[:], diff_a[:], factor, 0.0, ALU.mult, ALU.max)
+                add_term(n, relu_a)
 
-        def db(n):
-            diff_b = work.tile([P, PACK, WIDTHS[n]], F32, bufs=BT)
-            st[n]["db"] = diff_b
-            nc.vector.scalar_tensor_tensor(
-                diff_b[:].rearrange(flat), st[n]["yc"][:].rearrange(flat), -SPREAD, st[n]["yb4"][:].rearrange(flat), ALU.mult, ALU.add
-            )
-
-        def sa(n):
-            term_a = work.tile([P, PACK, WIDTHS[n]], F32, bufs=BT)
-            nc.vector.scalar_tensor_tensor(
-                term_a[:].rearrange(flat), st[n]["da"][:].rearrange(flat), st[n]["ka"] / SPREAD, w_t[n][:, 0].rearrange(flat), ALU.mult, ALU.mult
-            )
-            add_term(n, term_a)
-            add_term(n, st[n]["yc"])
-
-        def sb(n):
-            term_b = work.tile([P, PACK, WIDTHS[n]], F32, bufs=BT)
-            nc.vector.scalar_tensor_tensor(
-                term_b[:].rearrange(flat), st[n]["db"][:].rearrange(flat), 1.0 / SPREAD, w_t[n][:, 1].rearrange(flat), ALU.mult, ALU.mult
-            )
+        def middle_terms(n):
+            term_b = chunk_tile(n, "term_b")
+            two_ops(term_b, held[n]["diff_b"], 1.0 / SPREAD, weights[n][:, 1], ALU.mult, ALU.mult)
             add_term(n, term_b)
+            extreme = chunk_tile(n, "extreme")
+            pick = ALU.max if six_terms(n) else ALU.min
+            two_ops(extreme, held[n]["diff_a"], held[n]["to_a"], held[n]["diff_b"], ALU.mult, pick)
+            if six_terms(n):
+                add_term(n, extreme)
 
-        def ra(n):
-            if n in FOUR:
-                return
-            above_a = work.tile([P, PACK, WIDTHS[n]], F32, bufs=BT)
-            if n in RAS:
-                nc.scalar.activation(above_a[:], st[n]["da"][:], ACT.Relu, scale=st[n]["ka"] * (-1.0 if n in SIX else 1.0))
+        def last_terms(n):
+            relu_b = chunk_tile(n, "relu_b")
+            if six_terms(n):
+                nc.vector.tensor_scalar(relu_b[:], held[n]["diff_b"][:], -1.0, 0.0, ALU.mult, ALU.max)
             else:
-                nc.vector.tensor_scalar(above_a[:], st[n]["da"][:], st[n]["ka"] * (-1.0 if n in SIX else 1.0), 0.0, ALU.mult, ALU.max)
-            st[n]["above_a"] = above_a
-            if n not in RAS:
-                add_term(n, above_a)
+                two_ops(relu_b, held[n]["diff_b"], 0.0, held[n]["extreme"], ALU.max, ALU.subtract)
+            add_term(n, relu_b, last=not relu_a_on_scalar(n))
+            if relu_a_on_scalar(n):
+                add_term(n, held[n]["relu_a"], last=True)
 
-        def rx(n):
-            if n in RAS and n not in FOUR:
-                add_term(n, st[n]["above_a"])
-            if n in RBS and n in SIX:
-                add_term(n, st[n]["part"])
-
-        def nn(n):
-            least = work.tile([P, PACK, WIDTHS[n]], F32, bufs=BT)
-            nc.vector.scalar_tensor_tensor(
-                least[:].rearrange(flat), st[n]["da"][:].rearrange(flat), st[n]["ka"], st[n]["db"][:].rearrange(flat), ALU.mult, ALU.max if n in SIX else ALU.min
-            )
-            st[n]["least"] = least
-            if n in SIX:
-                add_term(n, least)
-
-        def tt(n):
-            part = work.tile([P, PACK, WIDTHS[n]], F32, bufs=BT)
-            if n in SIX:
-                if n in RBS:
-                    nc.scalar.activation(part[:], st[n]["db"][:], ACT.Relu, scale=-1.0)
-                else:
-                    nc.vector.tensor_scalar(part[:], st[n]["db"][:], -1.0, 0.0, ALU.mult, ALU.max)
-                st[n]["part"] = part
-                if n not in RBS:
-                    add_term(n, part)
-                return
-            nc.vector.scalar_tensor_tensor(
-                part[:].rearrange(flat), st[n]["db"][:].rearrange(flat), 0.0, st[n]["least"][:].rearrange(flat), ALU.max, ALU.subtract
-            )
-            if n in FOUR:
-                above_a = work.tile([P, PACK, WIDTHS[n]], F32, bufs=BT)
-                nc.vector.scalar_tensor_tensor(
-                    above_a[:].rearrange(flat), st[n]["da"][:].rearrange(flat), 0.0, part[:].rearrange(flat), ALU.max, ALU.add
+        def scale_and_turn(n):
+            turned = small.tile([P, WIDTHS[n] // P, 2, P], F32, tag="turned", name="turned")
+            for b, bank in enumerate(held[n]["banks"]):
+                hid_t = late.tile([P, 2, P, 2], BF16, align_bytes=64)
+                nc.vector.tensor_tensor(
+                    hid_t[:], bank[:].rearrange("r (p u e) -> r u p e", u=2, e=2), unit_row[:], ALU.mult
                 )
-                part = above_a
-            add_term(n, part)
+                pairs = hid_t[:].rearrange("r u p e -> r (u p e)").bitcast(F32)
+                for u in range(2):
+                    nc.tensor.transpose(turned[:, b, u, :], pairs[:, P * u : P * (u + 1)], ident[:])
+            held[n]["turned"] = turned
 
-        def turn(n, b):
-            acc = st[n]["acc"][b]
-            hid_t = late.tile([P, 2, P, 2], BF16, align_bytes=64, bufs=BL)
-            nc.vector.tensor_tensor(
-                hid_t[:], acc[:].rearrange("r (p u e) -> r u p e", u=2, e=2), unit_row[:], ALU.mult
-            )
-            pairs = hid_t[:].rearrange("r u p e -> r (u p e)").bitcast(F32)
-            for u in range(2):
-                nc.tensor.transpose(st[n]["back"][:, b, u, :], pairs[:, P * u : P * (u + 1)], ident[:])
-
-        def tn(n):
-            st[n]["back"] = small.tile([P, WIDTHS[n] // P, 2, P], F32, tag="back", name="back")
-            for b in range(WIDTHS[n] // P):
-                turn(n, b)
-
-        def hc(n):
-            hid = late.tile([P, WIDTHS[n] * PACK], BF16, align_bytes=64, bufs=BL)
-            (nc.scalar.copy if n in HS else nc.vector.tensor_copy)(
+        def copy_words(n):
+            hid = late.tile([P, WIDTHS[n] * PACK], BF16, align_bytes=64)
+            copy = nc.scalar.copy if SCALAR_WORD_COPY_FROM <= n < CHUNKS - 1 else nc.vector.tensor_copy
+            copy(
                 hid[:].bitcast(F32).rearrange("p (b r u) -> p b r u", b=WIDTHS[n] // P, u=2),
-                st[n]["back"][:].rearrange("p b u r -> p b r u"),
+                held[n]["turned"][:].rearrange("p b u r -> p b r u"),
             )
-            st[n]["hid"] = hid
+            held[n]["hid"] = hid
 
-        def pr(n):
+        def second_product(n):
             width = WIDTHS[n]
-            hid_codes = late.tile([P, width], U32, align_bytes=64, bufs=BL)
-            hid_scales = late.tile([P, width], U8, align_bytes=64, bufs=BL)
-            nc.vector.quantize_mx(out=hid_codes[:].bitcast(FP8X4), scales=hid_scales[:], in_=st[n]["hid"][:])
-            st[n]["res_ps"] = []
-            for b in range(width // P):
-                sub = slice(P * b, P * (b + 1))
+            hid_codes = late.tile([P, width], U32, align_bytes=64)
+            hid_scales = late.tile([P, width], U8, align_bytes=64)
+            nc.vector.quantize_mx(out=hid_codes[:].bitcast(FP8X4), scales=hid_scales[:], in_=held[n]["hid"][:])
+            blocks = [slice(P * b, P * (b + 1)) for b in range(width // P)]
+            results = []
+            for block in blocks:
                 res_ps = small.tile([P, PACK, P], F32, tag="res", name="res_ps")
                 for t in range(PACK):
                     nc.tensor.matmul_mx(
                         out=res_ps[:, t, :],
-                        lhsT=w2_t[:, t, :, :].rearrange("p m b -> p (m b)").bitcast(FP4X4),
+                        lhsT=w2_t[:, t, :, :].rearrange("p c b -> p (c b)").bitcast(FP4X4),
                         lhsT_scale=w2s_t[:, t, :],
-                        rhs=hid_codes[:, sub].bitcast(FP8X4),
-                        rhs_scale=hid_scales[:, sub],
+                        rhs=hid_codes[:, block].bitcast(FP8X4),
+                        rhs_scale=hid_scales[:, block],
                         start=True,
                         stop=True,
                     )
-                st[n]["res_ps"].append(res_ps)
+                results.append(res_ps)
+            res = late.tile([P, PACK, width], F32)
+            res16 = late.tile([P, width, PACK], BF16, align_bytes=64)
+            for block, res_ps in zip(blocks, results):
+                nc.scalar.copy(res16[:, block, :], res_ps[:].rearrange("p t r -> p r t"))
+                nc.scalar.copy(res[:, :, block], res_ps[:])
+            nc.sync.dma_start(out=out_rows[:, :, STARTS[n] : STARTS[n] + width], in_=res[:])
+            held[n]["res16"] = res16
 
-        def rs(n):
-            width = WIDTHS[n]
-            cols = slice(starts[n], starts[n] + width)
-            res = late.tile([P, PACK, width], F32, bufs=BL)
-            res16 = late.tile([P, width, PACK], BF16, align_bytes=64, bufs=BL)
-            for b, res_ps in enumerate(st[n]["res_ps"]):
-                sub = slice(P * b, P * (b + 1))
-                if R16 == "S" or n in RS:
-                    nc.scalar.copy(res16[:, sub, :], res_ps[:].rearrange("p t r -> p r t"))
-                nc.scalar.copy(res[:, :, sub], res_ps[:])
-            nc.sync.dma_start(out=out_rows[:, :, cols], in_=res[:])
-            st[n]["res16"] = res16
-            st[n]["res"] = res
-
-        def pl(n):
-            width = WIDTHS[n]
-            cols = slice(starts[n], starts[n] + width)
-            if not (R16 == "S" or n in RS):
-                nc.vector.tensor_copy(st[n]["res16"][:], st[n]["res"][:].rearrange("p t r -> p r t"))
-            out_codes = late.tile([P, width], U32, align_bytes=64, bufs=BL)
+        def make_planes(n):
+            cols = slice(STARTS[n], STARTS[n] + WIDTHS[n])
+            out_codes = late.tile([P, WIDTHS[n]], U32, align_bytes=64)
             nc.vector.quantize_mx(
-                out=out_codes[:].bitcast(FP8X4), scales=out_scales[:, cols], in_=st[n]["res16"][:].rearrange("p r t -> p (r t)")
+                out=out_codes[:].bitcast(FP8X4),
+                scales=out_scales[:, cols],
+                in_=held[n]["res16"][:].rearrange("p r t -> p (r t)"),
             )
             nc.sync.dma_start(out=out_words[:, cols], in_=out_codes[:].bitcast(I32))
 
-        stage = dict(rx=rx, gc=gc, ga=ga, gb=gb, da=da, db=db, sa=sa, sb=sb, ra=ra, nn=nn, tt=tt, tn=tn, hc=hc, pr=pr, rs=rs, pl=pl)
-        for step in range(-2, len(WIDTHS) + 5):
-            for key in (LAST if step >= len(WIDTHS) - NL else ORDER).split():
-                n = step - int(key[2:])
-                if 0 <= n < len(WIDTHS):
-                    stage[key[:2]](n)
+        for step in range(-1, CHUNKS + PLANES_LAG):
+            if step < CHUNKS and (step < 0 or WIDTHS[step] == WIDE):
+                order = [(scalar_gathers, 1), (first_terms, 0), (scale_and_turn, -1), (middle_terms, 0)]
+                order += [(copy_words, -1), (last_terms, 0)]
+            else:
+                order = [(scalar_gathers, 1), (first_terms, 0), (middle_terms, 0), (last_terms, 0)]
+                order += [(scale_and_turn, -1), (copy_words, -1)]
+            for part, ahead in order + [(second_product, -1), (make_planes, -PLANES_LAG)]:
+                if 0 <= step + ahead < CHUNKS:
+                    part(step + ahead)
 
         for quad in range(4):
-            (nc.sync if quad % 2 else nc.scalar).dma_start(
+            queue = nc.sync if quad % 2 else nc.scalar
+            queue.dma_start(
                 out=out_2[0, 4 * quad : 4 * quad + 4, :].bitcast(I32),
                 in_=out_scales[32 * quad : 32 * quad + 4, :].bitcast(I32),
             )

@@ -27,11 +27,11 @@ WIDE, NARROW = 2 * P, P
 WIDTHS = (WIDE, WIDE, WIDE, NARROW, NARROW)
 CHUNKS = len(WIDTHS)
 STARTS = tuple(sum(WIDTHS[:n]) for n in range(CHUNKS))
+LAST = CHUNKS - 1
 VECTOR_GATHERS_A_BELOW = 2
-SCALAR_RELU_FROM = 1
 SCALAR_WORD_COPY_FROM = 2
 SCALAR_COPIES_Y_BELOW = 2
-PLANES_LAG = 3
+PLANES_LAG = 4
 
 
 def load_scale_rows(nc, scale_tile, rows):
@@ -151,12 +151,6 @@ def tile_picked_ybaryin_rng_po_kernel(
                 out[:].rearrange(FLAT), in0[:].rearrange(FLAT), scalar, in1[:].rearrange(FLAT), op0, op1
             )
 
-        def six_terms(n):
-            return WIDTHS[n] == WIDE
-
-        def relu_a_on_scalar(n):
-            return SCALAR_RELU_FROM <= n < CHUNKS - 1
-
         def add_term(n, term, first=False, last=False):
             for b, bank in enumerate(held[n]["banks"]):
                 for t in range(PACK):
@@ -190,37 +184,32 @@ def tile_picked_ybaryin_rng_po_kernel(
                 to_a = 1.0
             held[n]["to_a"] = to_a
             held[n]["banks"] = [sums.tile([P, H], F32, tag="sum", name="bank") for b in range(WIDTHS[n] // P)]
+            if n < LAST:
+                add_term(n, yc, first=True)
             term_a = chunk_tile(n, "term_a")
             two_ops(term_a, diff_a, to_a / SPREAD, weights[n][:, 0], ALU.mult, ALU.mult)
-            add_term(n, term_a, first=True)
-            add_term(n, yc)
+            add_term(n, term_a, first=n == LAST)
+            if n == LAST:
+                add_term(n, yc)
             two_ops(chunk_tile(n, "diff_b"), yc, -SPREAD, held[n]["yb4"], ALU.mult, ALU.add)
             relu_a = chunk_tile(n, "relu_a")
-            factor = -to_a if six_terms(n) else to_a
-            if relu_a_on_scalar(n):
-                nc.scalar.activation(relu_a[:], diff_a[:], ACT.Relu, scale=factor)
+            if n < LAST:
+                nc.scalar.activation(relu_a[:], diff_a[:], ACT.Relu, scale=to_a)
             else:
-                nc.vector.tensor_scalar(relu_a[:], diff_a[:], factor, 0.0, ALU.mult, ALU.max)
+                nc.vector.tensor_scalar(relu_a[:], diff_a[:], to_a, 0.0, ALU.mult, ALU.max)
                 add_term(n, relu_a)
 
         def middle_terms(n):
             term_b = chunk_tile(n, "term_b")
             two_ops(term_b, held[n]["diff_b"], 1.0 / SPREAD, weights[n][:, 1], ALU.mult, ALU.mult)
             add_term(n, term_b)
-            extreme = chunk_tile(n, "extreme")
-            pick = ALU.max if six_terms(n) else ALU.min
-            two_ops(extreme, held[n]["diff_a"], held[n]["to_a"], held[n]["diff_b"], ALU.mult, pick)
-            if six_terms(n):
-                add_term(n, extreme)
+            two_ops(chunk_tile(n, "least"), held[n]["diff_a"], held[n]["to_a"], held[n]["diff_b"], ALU.mult, ALU.min)
 
         def last_terms(n):
-            relu_b = chunk_tile(n, "relu_b")
-            if six_terms(n):
-                nc.vector.tensor_scalar(relu_b[:], held[n]["diff_b"][:], -1.0, 0.0, ALU.mult, ALU.max)
-            else:
-                two_ops(relu_b, held[n]["diff_b"], 0.0, held[n]["extreme"], ALU.max, ALU.subtract)
-            add_term(n, relu_b, last=not relu_a_on_scalar(n))
-            if relu_a_on_scalar(n):
+            rest = chunk_tile(n, "rest")
+            two_ops(rest, held[n]["diff_b"], 0.0, held[n]["least"], ALU.max, ALU.subtract)
+            add_term(n, rest, last=n == LAST)
+            if n < LAST:
                 add_term(n, held[n]["relu_a"], last=True)
 
         def scale_and_turn(n):
@@ -237,7 +226,7 @@ def tile_picked_ybaryin_rng_po_kernel(
 
         def copy_words(n):
             hid = late.tile([P, WIDTHS[n] * PACK], BF16, align_bytes=64)
-            copy = nc.scalar.copy if SCALAR_WORD_COPY_FROM <= n < CHUNKS - 1 else nc.vector.tensor_copy
+            copy = nc.scalar.copy if SCALAR_WORD_COPY_FROM <= n < LAST else nc.vector.tensor_copy
             copy(
                 hid[:].bitcast(F32).rearrange("p (b r u) -> p b r u", b=WIDTHS[n] // P, u=2),
                 held[n]["turned"][:].rearrange("p b u r -> p b r u"),

from contextlib import ExitStack

import concourse.mybir as mybir
from concourse.masks import make_identity

K, T, S, N, H, U = 512, 2048, 512, 512, 512, 1024
FLOPS = 2 * K * N * S + 2 * H * N * U

F32 = mybir.dt.float32
BF16 = mybir.dt.bfloat16
I32 = mybir.dt.int32
U32 = mybir.dt.uint32
U16 = mybir.dt.uint16
U8 = mybir.dt.uint8
FP8X4 = mybir.dt.float8_e4m3fn_x4
FP4X4 = mybir.dt.float4_e2m1fn_x4
ALU = mybir.AluOpType
ACT = mybir.ActivationFunctionType

P = 128
PACK = 4
LIST_ROWS = 16
SPREAD = 0.4
FLAT = "p t r -> p (t r)"

WIDE, NARROW = 2 * P, P
WIDTHS = (WIDE, WIDE, WIDE, NARROW, NARROW)
CHUNKS = len(WIDTHS)
STARTS = tuple(sum(WIDTHS[:n]) for n in range(CHUNKS))
LAST = CHUNKS - 1
VECTOR_GATHERS_A_BELOW = 2
SCALAR_WORD_COPY_FROM = 2
SCALAR_COPIES_Y_BELOW = 2
PLANES_LAG = 4


def load_scale_rows(nc, scale_tile, rows):
    for quad in range(4):
        nc.sync.dma_start(
            out=scale_tile[32 * quad : 32 * quad + 4, :].bitcast(I32),
            in_=rows[0, 4 * quad : 4 * quad + 4, :].bitcast(I32),
        )


def tile_picked_ybaryin_rng_po_kernel(
    tc, x_words, x_scales, w1_words, w1_scales, wa, wb, unit, w2_words, w2_scales, offs, va, vb, vc, out_0, out_1, out_2
):
    nc = tc.nc
    with ExitStack() as ctx:
        keep = ctx.enter_context(tc.tile_pool(name="keep", bufs=1))
        work = ctx.enter_context(tc.tile_pool(name="work", bufs=2))
        late = ctx.enter_context(tc.tile_pool(name="late", bufs=PLANES_LAG + 1))
        sums = ctx.enter_context(tc.psum_pool(name="sums", bufs=4))
        small = ctx.enter_context(tc.psum_pool(name="small", bufs=2))

        offs_t = keep.tile([P, S // LIST_ROWS], U16)
        va_t = keep.tile([P, U // LIST_ROWS], U16)
        vb_t = keep.tile([P, U // LIST_ROWS], U16)
        vc_t = keep.tile([P, U // LIST_ROWS], U16)
        x_tab = keep.tile([P, T], U32, align_bytes=64)
        xs_tab = keep.tile([P, T], U8, align_bytes=64)
        w1_t = keep.tile([P, 2 * N], U8, align_bytes=64)
        w1s_t = keep.tile([P, N], U8, align_bytes=64)
        w2_raw = keep.tile([P, 2 * N], U8, align_bytes=64)
        w2s_raw = keep.tile([P, N], U8, align_bytes=64)
        unit_t = keep.tile([P, PACK], F32)

        nc.gpsimd.memset(xs_tab[:].bitcast(I32), 0)
        nc.vector.memset(w1s_t[:].bitcast(I32), 0)
        nc.vector.memset(w2s_raw[:].bitcast(I32), 0)

        nc.sync.dma_start(offs_t[:], offs)
        nc.sync.dma_start(out=unit_t[:], in_=unit.rearrange("(p j) o -> p (j o)", j=PACK))
        nc.sync.dma_start(out=w2_raw[:].bitcast(I32), in_=w2_words[0].bitcast(I32))
        load_scale_rows(nc, xs_tab, x_scales)
        nc.sync.dma_start(out=x_tab[:].bitcast(I32), in_=x_words[0].rearrange("p c r -> p (c r)").bitcast(I32))
        nc.sync.dma_start(out=w1_t[:].bitcast(I32), in_=w1_words[0].bitcast(I32))
        load_scale_rows(nc, w1s_t, w1_scales)
        nc.sync.dma_start(vc_t[:], vc)
        nc.sync.dma_start(va_t[:], va)
        nc.sync.dma_start(vb_t[:], vb)

        wa_rows = wa.rearrange("(t p) r -> p t r", p=P)
        wb_rows = wb.rearrange("(t p) r -> p t r", p=P)
        weights = []
        for n in range(CHUNKS):
            cols = slice(STARTS[n], STARTS[n] + WIDTHS[n])
            weights.append(keep.tile([P, 2, PACK, WIDTHS[n]], F32, name=f"weights{n}"))
            nc.sync.dma_start(out=weights[n][:, 0], in_=wa_rows[:, :, cols])
            nc.sync.dma_start(out=weights[n][:, 1], in_=wb_rows[:, :, cols])
            if n == 0:
                load_scale_rows(nc, w2s_raw, w2_scales)

        ident = keep.tile([P, P], F32)
        make_identity(nc, ident[:])

        unit_ps = small.tile([P, PACK, P], F32, tag="res", name="unit_ps")
        for j in range(PACK):
            nc.tensor.transpose(unit_ps[:, j, :], unit_t[:, j : j + 1].to_broadcast([P, P]), ident[:])
        unit_row = keep.tile([P, 2, P, 2], F32)
        nc.scalar.copy(unit_row[:], unit_ps[:].rearrange("r (u e) p -> r u p e", e=2))

        xs_g = keep.tile([P, S], U8, align_bytes=64)
        x_g = keep.tile([P, S], U32, align_bytes=64)
        nc.vector.tensor_copy(xs_g[:], xs_tab[:].indirect(offs_t[:]))
        half = S // 2
        halves = [slice(0, half), slice(half, S)]
        for picked in halves:
            offsets = offs_t[:, picked.start // LIST_ROWS : picked.stop // LIST_ROWS]
            nc.vector.tensor_copy(x_g[:, picked], x_tab[:].indirect(offsets))

        y = []
        for t in range(PACK):
            y_ps = sums.tile([P, S], F32, tag="sum", name="y_ps")
            for picked in halves:
                nc.tensor.matmul_mx(
                    out=y_ps[:, picked],
                    lhsT=w1_t[:, 2 * P * t : 2 * P * (t + 1)].bitcast(FP4X4),
                    lhsT_scale=w1s_t[:, P * t : P * (t + 1)],
                    rhs=x_g[:, picked].bitcast(FP8X4),
                    rhs_scale=xs_g[:, picked],
                    start=True,
                    stop=True,
                )
            y.append(keep.tile([P, S], F32, name=f"y{t}"))
            if t < SCALAR_COPIES_Y_BELOW:
                nc.scalar.copy(y[t][:], y_ps[:])
            else:
                nc.vector.tensor_copy(y[t][:], y_ps[:])

        w2_t = keep.tile([P, PACK, P, 2], U8, align_bytes=64)
        w2s_t = keep.tile([P, PACK, P], U8, align_bytes=64)
        nc.vector.tensor_copy(w2_t[:], w2_raw[:].rearrange("p (c t b) -> p t c b", t=PACK, b=2))
        nc.vector.tensor_copy(w2s_t[:], w2s_raw[:].rearrange("p (c t) -> p t c", t=PACK))

        out_scales = keep.tile([P, U], U8, align_bytes=64)
        out_rows = out_0.rearrange("(p t) r -> p t r", t=PACK)
        out_words = out_1[0].rearrange("p c r -> p (c r)").bitcast(I32)

        held = [{} for n in range(CHUNKS)]

        def chunk_tile(n, name):
            held[n][name] = work.tile([P, PACK, WIDTHS[n]], F32, name=name)
            return held[n][name]

        def looked_up(n, t, list_tile):
            return y[t][:].indirect(list_tile[:, STARTS[n] // LIST_ROWS : (STARTS[n] + WIDTHS[n]) // LIST_ROWS])

        def two_ops(out, in0, scalar, in1, op0, op1):
            nc.vector.scalar_tensor_tensor(
                out[:].rearrange(FLAT), in0[:].rearrange(FLAT), scalar, in1[:].rearrange(FLAT), op0, op1
            )

        def add_term(n, term, first=False, last=False):
            for b, bank in enumerate(held[n]["banks"]):
                for t in range(PACK):
                    nc.tensor.matmul(
                        bank[:, P * t : P * (t + 1)],
                        term[:, t, P * b : P * (b + 1)],
                        ident[:],
                        start=(first and t == 0),
                        stop=(last and t == PACK - 1),
                        is_transpose=True,
                    )

        def scalar_gathers(n):
            wanted = [("yc", vc_t, 1.0), ("ya4", va_t, SPREAD), ("yb4", vb_t, SPREAD)]
            for name, list_tile, factor in wanted:
                if name == "ya4" and n < VECTOR_GATHERS_A_BELOW:
                    continue
                corner = chunk_tile(n, name)
                for t in range(PACK):
                    nc.scalar.activation(corner[:, t, :], looked_up(n, t, list_tile), ACT.Copy, scale=factor)

        def first_terms(n):
            yc = held[n]["yc"]
            diff_a = chunk_tile(n, "diff_a")
            if n < VECTOR_GATHERS_A_BELOW:
                for t in range(PACK):
                    nc.vector.tensor_tensor(diff_a[:, t, :], looked_up(n, t, va_t), yc[:, t, :], ALU.subtract)
                to_a = SPREAD
            else:
                two_ops(diff_a, yc, -SPREAD, held[n]["ya4"], ALU.mult, ALU.add)
                to_a = 1.0
            held[n]["to_a"] = to_a
            held[n]["banks"] = [sums.tile([P, H], F32, tag="sum", name="bank") for b in range(WIDTHS[n] // P)]
            if n < LAST:
                add_term(n, yc, first=True)
            term_a = chunk_tile(n, "term_a")
            two_ops(term_a, diff_a, to_a / SPREAD, weights[n][:, 0], ALU.mult, ALU.mult)
            add_term(n, term_a, first=n == LAST)
            if n == LAST:
                add_term(n, yc)
            two_ops(chunk_tile(n, "diff_b"), yc, -SPREAD, held[n]["yb4"], ALU.mult, ALU.add)
            relu_a = chunk_tile(n, "relu_a")
            if n < LAST:
                nc.scalar.activation(relu_a[:], diff_a[:], ACT.Relu, scale=to_a)
            else:
                nc.vector.tensor_scalar(relu_a[:], diff_a[:], to_a, 0.0, ALU.mult, ALU.max)
                add_term(n, relu_a)

        def middle_terms(n):
            term_b = chunk_tile(n, "term_b")
            two_ops(term_b, held[n]["diff_b"], 1.0 / SPREAD, weights[n][:, 1], ALU.mult, ALU.mult)
            add_term(n, term_b)
            two_ops(chunk_tile(n, "least"), held[n]["diff_a"], held[n]["to_a"], held[n]["diff_b"], ALU.mult, ALU.min)

        def last_terms(n):
            rest = chunk_tile(n, "rest")
            two_ops(rest, held[n]["diff_b"], 0.0, held[n]["least"], ALU.max, ALU.subtract)
            add_term(n, rest, last=n == LAST)
            if n < LAST:
                add_term(n, held[n]["relu_a"], last=True)

        def scale_and_turn(n):
            turned = small.tile([P, WIDTHS[n] // P, 2, P], F32, tag="turned", name="turned")
            for b, bank in enumerate(held[n]["banks"]):
                hid_t = late.tile([P, 2, P, 2], BF16, align_bytes=64)
                nc.vector.tensor_tensor(
                    hid_t[:], bank[:].rearrange("r (p u e) -> r u p e", u=2, e=2), unit_row[:], ALU.mult
                )
                pairs = hid_t[:].rearrange("r u p e -> r (u p e)").bitcast(F32)
                for u in range(2):
                    nc.tensor.transpose(turned[:, b, u, :], pairs[:, P * u : P * (u + 1)], ident[:])
            held[n]["turned"] = turned

        def copy_words(n):
            hid = late.tile([P, WIDTHS[n] * PACK], BF16, align_bytes=64)
            copy = nc.scalar.copy if SCALAR_WORD_COPY_FROM <= n < LAST else nc.vector.tensor_copy
            copy(
                hid[:].bitcast(F32).rearrange("p (b r u) -> p b r u", b=WIDTHS[n] // P, u=2),
                held[n]["turned"][:].rearrange("p b u r -> p b r u"),
            )
            held[n]["hid"] = hid

        def second_product(n):
            width = WIDTHS[n]
            hid_codes = late.tile([P, width], U32, align_bytes=64)
            hid_scales = late.tile([P, width], U8, align_bytes=64)
            nc.vector.quantize_mx(out=hid_codes[:].bitcast(FP8X4), scales=hid_scales[:], in_=held[n]["hid"][:])
            blocks = [slice(P * b, P * (b + 1)) for b in range(width // P)]
            results = []
            for block in blocks:
                res_ps = small.tile([P, PACK, P], F32, tag="res", name="res_ps")
                for t in range(PACK):
                    nc.tensor.matmul_mx(
                        out=res_ps[:, t, :],
                        lhsT=w2_t[:, t, :, :].rearrange("p c b -> p (c b)").bitcast(FP4X4),
                        lhsT_scale=w2s_t[:, t, :],
                        rhs=hid_codes[:, block].bitcast(FP8X4),
                        rhs_scale=hid_scales[:, block],
                        start=True,
                        stop=True,
                    )
                results.append(res_ps)
            res = late.tile([P, PACK, width], F32)
            res16 = late.tile([P, width, PACK], BF16, align_bytes=64)
            for block, res_ps in zip(blocks, results):
                nc.scalar.copy(res16[:, block, :], res_ps[:].rearrange("p t r -> p r t"))
                nc.scalar.copy(res[:, :, block], res_ps[:])
            nc.sync.dma_start(out=out_rows[:, :, STARTS[n] : STARTS[n] + width], in_=res[:])
            held[n]["res16"] = res16

        def make_planes(n):
            cols = slice(STARTS[n], STARTS[n] + WIDTHS[n])
            out_codes = late.tile([P, WIDTHS[n]], U32, align_bytes=64)
            nc.vector.quantize_mx(
                out=out_codes[:].bitcast(FP8X4),
                scales=out_scales[:, cols],
                in_=held[n]["res16"][:].rearrange("p r t -> p (r t)"),
            )
            nc.sync.dma_start(out=out_words[:, cols], in_=out_codes[:].bitcast(I32))

        for step in range(-1, CHUNKS + PLANES_LAG):
            if step < CHUNKS and (step < 0 or WIDTHS[step] == WIDE):
                order = [(scalar_gathers, 1), (first_terms, 0), (scale_and_turn, -1), (middle_terms, 0)]
                order += [(copy_words, -1), (last_terms, 0)]
            else:
                order = [(scalar_gathers, 1), (first_terms, 0), (middle_terms, 0), (last_terms, 0)]
                order += [(scale_and_turn, -1), (copy_words, -1)]
            for part, ahead in order + [(second_product, -1), (make_planes, -PLANES_LAG)]:
                if 0 <= step + ahead < CHUNKS:
                    part(step + ahead)

        for quad in range(4):
            queue = nc.sync if quad % 2 else nc.scalar
            queue.dma_start(
                out=out_2[0, 4 * quad : 4 * quad + 4, :].bitcast(I32),
                in_=out_scales[32 * quad : 32 * quad + 4, :].bitcast(I32),
            )
